import numpy as np
import ml_dtypes


def mxq(x, axis, fmt="e4m3"):
    dtype, down = {"e4m3": (ml_dtypes.float8_e4m3fn, 7), "e5m2": (ml_dtypes.float8_e5m2, 14)}[fmt]
    v = np.moveaxis(np.asarray(x, np.float32).astype(ml_dtypes.bfloat16).astype(np.float64), axis, -1)
    blocks = v.reshape(v.shape[:-1] + (-1, 32))
    amax = np.abs(blocks).max(-1, keepdims=True)
    byte = np.maximum(np.where(amax > 0, np.frexp(amax)[1] - 1 + 127, 0) - down, 1)
    scale = np.exp2(byte - 127.0)
    codes = (blocks / scale).astype(np.float32).astype(dtype).astype(np.float64)
    return np.moveaxis((codes * scale).reshape(v.shape), -1, axis)


WIDE = False


def mx_kscale(k):
    if not WIDE:
        return np.ones(k)
    levels = np.array([10, -10, 5, -5, 0])
    if k % 512:
        return np.exp2(np.random.permutation(np.resize(levels, k // 32))).repeat(32)
    a = np.empty((k // 512, 16))
    for p in range(k // 512):
        a[p, :8] = np.random.permutation(np.resize(levels, 8))
        for g in range(8):
            far = levels[np.abs(levels - a[p, g]) >= 10]
            a[p, g + 8] = far[np.random.randint(len(far))]
    return np.exp2(a.ravel()).repeat(32)


BF16 = ml_dtypes.bfloat16


def bf(x):
    return np.asarray(x, np.float32).astype(BF16)


def f64(x):
    return np.asarray(x).astype(np.float64)


E2M1 = np.array([0.0, 0.5, 1.0, 1.5, 2.0, 3.0, 4.0, 6.0, -0.0, -0.5, -1.0, -1.5, -2.0, -3.0, -4.0, -6.0])


def pack_weight(w, fmt):
    k, n = w.shape
    w = f64(bf(w)).reshape(k // 32, 32, n)
    amax = np.abs(w).max(1)
    if fmt == "e4m3":
        byte = np.frexp(amax)[1] - 1 + 127 - 7
    else:
        mant, ex = np.frexp(amax / 6.0)
        byte = np.where(mant > 0.5, ex, ex - 1) + 127
    byte = np.clip(np.where(amax > 0, byte, 1), 1, 254)
    scaled = (w * np.exp2(127.0 - byte)[:, None, :]).reshape(k, n).astype(np.float32)
    by_word = np.ascontiguousarray(scaled.reshape(k // 512, 128, 4, n).transpose(0, 1, 3, 2))
    if fmt == "e4m3":
        words = by_word.astype(ml_dtypes.float8_e4m3fn).view(np.uint8)
    else:
        c = by_word.astype(ml_dtypes.float4_e2m1fn).view(np.uint8) & 0xF
        words = c[..., 0::2] | (c[..., 1::2] << 4)
    return np.ascontiguousarray(words), np.ascontiguousarray(byte.astype(np.uint8).reshape(k // 512, 16, n))


def unpack_weight(words, scales, fmt):
    g, p, n, _ = words.shape
    if fmt == "e4m3":
        vals = np.ascontiguousarray(words).view(ml_dtypes.float8_e4m3fn).astype(np.float64)
    else:
        nib = np.empty((g, p, n, 4), np.uint8)
        nib[..., 0::2] = words & 0xF
        nib[..., 1::2] = words >> 4
        vals = E2M1[nib]
    vals = vals * np.repeat(np.exp2(scales.astype(np.float64) - 127.0), 8, axis=1)[..., None]
    return vals.transpose(0, 1, 3, 2).reshape(g * 512, n)
def pack4(w):
    words, scales = pack_weight(w, "e2m1")
    return words.reshape(words.shape[0], 128, -1), scales


def unpack4(words, scales):
    return unpack_weight(words.reshape(words.shape[0], 128, -1, 2), scales, "e2m1")


def planes(Y):
    n, m = Y.shape
    b = f64(bf(Y)).reshape(n // 32, 32, m)
    amax = np.abs(b).max(1)
    byte = np.clip(np.where(amax > 0, np.frexp(amax)[1] - 1 + 127 - 7, 1), 1, 254)
    codes = (b * np.exp2(127.0 - byte)[:, None, :]).reshape(n, m).astype(np.float32).astype(ml_dtypes.float8_e4m3fn).view(np.uint8)
    words = codes.reshape(n // 512, 128, 4, m).transpose(0, 1, 3, 2)
    return np.ascontiguousarray(words), np.ascontiguousarray(byte.astype(np.uint8).reshape(n // 512, 16, m))


B, T, D, H, HD = 3, 1024, 2048, 4, 128


def setup_inputs():
    s = mx_kscale(D)
    size = np.exp(0.7 * np.random.randn(B * T, 1))
    x = np.random.randn(B * T, D) * size
    x_words, x_scales = pack_weight(x.T * s[:, None], "e4m3")
    w_v = np.random.randn(D, H * HD) / np.sqrt(D)
    b_v = 0.5 * np.random.randn(H * HD)
    return {
        "x_words": x_words,
        "x_scales": x_scales,
        "w_v": bf(w_v / s[:, None]),
        "b_v": bf(b_v),
    }


def reference(x_words, x_scales, w_v, b_v):
    xt = unpack_weight(x_words, x_scales, "e4m3")
    wq = mxq(f64(w_v), 0, "e4m3")
    v = (xt.T @ wq) + f64(b_v)
    y = v.reshape(B, T, H, HD).transpose(0, 2, 1, 3)
    Y = y.transpose(2, 0, 1, 3).reshape(T, B * H * HD)
    words, scales = planes(Y)
    return y, words, scales

@@ -1,0 +1,254 @@
+from contextlib import ExitStack
+
+import concourse.mybir as mybir
+from concourse.masks import make_identity
+
+B, T, D, H, HD = 3, 1024, 2048, 4, 128
+N = H * HD
+FLOPS = 2 * B * T * D * N
+
+F32 = mybir.dt.float32
+BF16 = mybir.dt.bfloat16
+I32 = mybir.dt.int32
+U8 = mybir.dt.uint8
+FP8X4 = mybir.dt.float8_e4m3fn_x4
+
+P = 128
+PACK = 4
+SPAN = P * PACK
+PASSES = D // SPAN
+GROUPS = B * T // SPAN
+HALVES = T // SPAN
+QUADS = 4
+HEAD_GROUPS = 2
+W_VECTOR_COLS = 192
+WIDE = [(0, H, t, 1) for t in range(PACK)]
+LAST = [(0, 2, 0, 2), (0, 2, 2, 2), (2, 1, 0, PACK), (3, 1, 0, PACK)]
+
+
+def tile_value_cache_projection_g6_kernel(tc, x_words, x_scales, w_v, b_v, out_0, out_1, out_2):
+    nc = tc.nc
+    x_i32 = [x_words[g].rearrange("p n t -> p (n t)").bitcast(I32) for g in range(PASSES)]
+    x_all = x_words.rearrange("g p n t -> p g (n t)").bitcast(I32)
+    xs_i32 = x_scales.bitcast(I32)
+    head_tokens = HEAD_GROUPS * SPAN
+
+    with ExitStack() as ctx:
+        keep = ctx.enter_context(tc.tile_pool(name="keep", bufs=1))
+        flow = ctx.enter_context(tc.tile_pool(name="flow", bufs=1))
+        psum = ctx.enter_context(tc.psum_pool(name="psum", bufs=1))
+        ctx.enter_context(tc.manual_schedule())
+
+        def kept(shape, dtype, name):
+            return keep.tile(shape, dtype, name=name, align_bytes=64)
+
+        def bank(group, t):
+            slot = (group % 2) * PACK + t
+            return psum.tile([P, N], F32, name="acc%d_%d" % (group, t), tag="bank%d" % slot)
+
+        def load_scales(raw, first, count):
+            for q in range(QUADS):
+                nc.sync.dma_start(
+                    out=raw[32 * q : 32 * q + 16, :].bitcast(I32),
+                    in_=xs_i32[:, 4 * q : 4 * q + 4, first // 4 : (first + count) // 4],
+                )
+
+        def sort_scales(raw, first, group):
+            out = kept([P, SPAN], U8, "xs%d" % group)
+            nc.vector.tensor_copy(
+                out=out[:].rearrange("p (t m i) -> p m t i", t=PACK, i=16),
+                in_=raw[:, first : first + SPAN].rearrange("p (m i t) -> p m t i", t=PACK, i=16),
+            )
+            return out
+
+        def sort_words(src, name, passes):
+            out = kept([P, passes, SPAN], I32, name)
+            nc.vector.tensor_copy(
+                out=out[:].rearrange("p g (t m i) -> p g m t i", t=PACK, i=2),
+                in_=src.rearrange("p g (m i t) -> p g m t i", t=PACK, i=2),
+            )
+            return out
+
+        def load_w(g):
+            raw = kept([P, PACK, N], BF16, "w_raw%d" % g)
+            nc.sync.dma_start(out=raw[:], in_=w_v[SPAN * g : SPAN * (g + 1), :].rearrange("(p j) c -> p j c", j=PACK))
+            return raw
+
+        def group_w(raw, g):
+            grouped = kept([P, N, PACK], BF16, "w_grouped%d" % g)
+            lo, hi = slice(0, W_VECTOR_COLS), slice(W_VECTOR_COLS, N)
+            nc.scalar.copy(
+                out=grouped[:, hi, :].rearrange("p (c i) j -> p c j i", i=4),
+                in_=raw[:, :, hi].rearrange("p j (c i) -> p c j i", i=4),
+            )
+            nc.vector.tensor_copy(
+                out=grouped[:, lo, :].rearrange("p (c i) j -> p c j i", i=4),
+                in_=raw[:, :, lo].rearrange("p j (c i) -> p c j i", i=4),
+            )
+            return grouped
+
+        def quantize_w(grouped, g):
+            codes = kept([P, N], I32, "w_codes%d" % g)
+            scales = kept([P, N], U8, "w_scales%d" % g)
+            nc.vector.quantize_mx(out=codes[:].bitcast(FP8X4), scales=scales[:], in_=grouped[:].rearrange("p c j -> p (c j)"))
+            return codes, scales
+
+        def multiply(acc, x_pass, x_scale, piece, slot, g):
+            h0, heads, t0, slots = piece
+            tokens = slice(P * (t0 + slot), P * (t0 + slot + 1))
+            channels = slice(HD * h0, HD * (h0 + heads))
+            nc.tensor.matmul_mx(
+                out=acc[:, HD * heads * slot : HD * heads * (slot + 1)],
+                lhsT=x_pass[:, tokens].bitcast(FP8X4),
+                lhsT_scale=x_scale[4 * g :, tokens],
+                rhs=w_q[g][0][:, channels].bitcast(FP8X4),
+                rhs_scale=w_q[g][1][:, channels],
+                start=(g == 0),
+                stop=(g == PASSES - 1),
+            )
+
+        def add_bias(y, acc, piece):
+            h0, heads, t0, slots = piece
+            nc.vector.tensor_tensor(
+                out=y[:].rearrange("p h (t c) -> p h t c", t=PACK)[:, h0 : h0 + heads, t0 : t0 + slots, :],
+                in0=acc[:].rearrange("p (t h c) -> p h t c", t=slots, h=heads),
+                in1=bias[:, h0 : h0 + heads, :].unsqueeze(2).to_broadcast([P, heads, slots, HD]),
+                op=mybir.AluOpType.add,
+            )
+
+        def store_and_round(y, y_bf, group, h0, heads):
+            b, half = divmod(group, HALVES)
+            nc.sync.dma_start(
+                out=out_0[b, h0 : h0 + heads, SPAN * half : SPAN * (half + 1), :].rearrange("h (p t) c -> p h (t c)", t=PACK),
+                in_=y[:, h0 : h0 + heads, :],
+            )
+            nc.scalar.copy(
+                out=y_bf[:, h0 : h0 + heads, :].rearrange("p h (c i t) -> p h c t i", t=PACK, i=4),
+                in_=y[:, h0 : h0 + heads, :].rearrange("p h (t c i) -> p h c t i", t=PACK, i=4),
+            )
+
+        def quantize_y(y_bf, codes, group, h0, heads):
+            b, half = divmod(group, HALVES)
+            nc.vector.quantize_mx(
+                out=codes[:, HD * h0 : HD * (h0 + heads)].bitcast(FP8X4),
+                scales=y_scales[half][:, N * b + HD * h0 : N * b + HD * (h0 + heads)],
+                in_=y_bf[:, h0 : h0 + heads, :].rearrange("p h e -> p (h e)"),
+            )
+
+        def store_codes(codes, group, h0, heads):
+            b, half = divmod(group, HALVES)
+            words = out_1[half].rearrange("p m t -> p (m t)").bitcast(I32)
+            nc.sync.dma_start(
+                out=words[:, N * b + HD * h0 : N * b + HD * (h0 + heads)], in_=codes[:, HD * h0 : HD * (h0 + heads)]
+            )
+
+        def store_scales(half):
+            for q in range(QUADS):
+                queue = nc.scalar if (half == HALVES - 1 and q % 2 == 0) else nc.sync
+                queue.dma_start(
+                    out=out_2[half, 4 * q : 4 * q + 4, :].bitcast(I32),
+                    in_=y_scales[half][32 * q : 32 * q + 4, :].bitcast(I32),
+                )
+
+        xs_head = kept([P, head_tokens], U8, "xs_head")
+        xs_rest = kept([P, B * T - head_tokens], U8, "xs_rest")
+        nc.vector.memset(xs_head[:].bitcast(I32), 0)
+        nc.vector.memset(xs_rest[:].bitcast(I32), 0)
+        ident = kept([P, P], BF16, "ident")
+        make_identity(nc, ident[:])
+
+        b_cols = kept([P, PACK], BF16, "b_cols")
+        nc.sync.dma_start(out=b_cols[:], in_=b_v.rearrange("(n j) -> n j", j=PACK))
+        w_raw, x_head = [], []
+        for g in range(PASSES):
+            w_raw.append(load_w(g))
+            if g == 0:
+                load_scales(xs_head, 0, head_tokens)
+            raw = kept([P, head_tokens], I32, "x_head%d" % g)
+            nc.sync.dma_start(out=raw[:], in_=x_i32[g][:, 0:head_tokens])
+            x_head.append(raw)
+        load_scales(xs_rest, head_tokens, B * T - head_tokens)
+        x_raw = {}
+        for group in range(HEAD_GROUPS, GROUPS):
+            raw = kept([P, PASSES, SPAN], I32, "x_raw%d" % group)
+            nc.sync.dma_start(out=raw[:], in_=x_all[:, :, SPAN * group : SPAN * (group + 1)])
+            x_raw[group] = raw
+
+        spread = psum.tile([P, PACK, P], BF16, name="spread", tag="bank%d" % (2 * PACK - 1))
+        for j in range(PACK):
+            nc.tensor.transpose(spread[:, j, :], b_cols[:, j : j + 1].to_broadcast([P, P]), ident[:])
+        bias = kept([P, H, HD], F32, "bias")
+        nc.scalar.copy(out=bias[:].rearrange("p h (n j) -> p (h n) j", j=PACK), in_=spread[:].rearrange("p j n -> p n j"))
+
+        y_scales = [kept([P, B * N], U8, "y_scales%d" % half) for half in range(HALVES)]
+
+        w_q, x_scale, acc = {}, {}, {}
+        for g in range(PASSES):
+            grouped = group_w(w_raw[g], g)
+            if g == 0:
+                for group in range(HEAD_GROUPS):
+                    x_scale[group] = sort_scales(xs_head, SPAN * group, group)
+            x_pass = [
+                sort_words(x_head[g][:, SPAN * group : SPAN * (group + 1)].unsqueeze(1), "x_sorted%d_%d" % (group, g), 1)
+                for group in range(HEAD_GROUPS)
+            ]
+            w_q[g] = quantize_w(grouped, g)
+            for group in range(HEAD_GROUPS):
+                for t in range(PACK):
+                    if g == 0:
+                        acc[group, t] = bank(group, t)
+                    multiply(acc[group, t], x_pass[group][:, 0, :], x_scale[group], WIDE[t], 0, g)
+
+        x_sorted = {}
+
+        def prepare(group):
+            x_scale[group] = sort_scales(xs_rest, SPAN * (group - HEAD_GROUPS), group)
+            x_sorted[group] = sort_words(x_raw[group][:], "x_sorted%d" % group, PASSES)
+
+        def result_tiles(group):
+            y = flow.tile([P, H, SPAN], F32, name="y%d" % group, tag="y", bufs=4, align_bytes=64)
+            y_bf = flow.tile([P, H, SPAN], BF16, name="y_bf%d" % group, tag="y_bf", bufs=3, align_bytes=64)
+            return y, y_bf, kept([P, N], I32, "y_codes%d" % group)
+
+        def finish(group):
+            quantize_y(results[group][1], results[group][2], group, 0, H)
+            store_codes(results[group][2], group, 0, H)
+            if group == GROUPS - 2:
+                store_scales(0)
+
+        prepare(HEAD_GROUPS)
+        results = {}
+        last = GROUPS - 1
+        for group in range(last):
+            results[group] = result_tiles(group)
+            y, y_bf, codes = results[group]
+            ahead = group + HEAD_GROUPS
+            for t in range(PACK):
+                add_bias(y, acc[group, t], WIDE[t])
+                if ahead < GROUPS:
+                    acc[ahead, t] = bank(ahead, t)
+                    piece = LAST[t] if ahead == last else WIDE[t]
+                    for slot in range(piece[3]):
+                        for g in range(PASSES):
+                            multiply(acc[ahead, t], x_sorted[ahead][:, g, :], x_scale[ahead], piece, slot, g)
+                if t == 1 and ahead + 1 < GROUPS:
+                    prepare(ahead + 1)
+                if t == 2 and group > 0:
+                    finish(group - 1)
+            store_and_round(y, y_bf, group, 0, H)
+
+        y, y_bf, codes = result_tiles(last)
+        add_bias(y, acc[last, 0], LAST[0])
+        add_bias(y, acc[last, 1], LAST[1])
+        store_and_round(y, y_bf, last, 0, 2)
+        finish(last - 1)
+        add_bias(y, acc[last, 2], LAST[2])
+        store_and_round(y, y_bf, last, 2, 1)
+        quantize_y(y_bf, codes, last, 0, 2)
+        store_codes(codes, last, 0, 2)
+        add_bias(y, acc[last, 3], LAST[3])
+        store_and_round(y, y_bf, last, 3, 1)
+        quantize_y(y_bf, codes, last, 2, 1)
+        quantize_y(y_bf, codes, last, 3, 1)
+        store_codes(codes, last, 2, 2)
+        store_scales(1)

@@ -21,8 +21,11 @@ GROUPS = B * T // SPAN
 HALVES = T // SPAN
 QUADS = 4
 HEAD_GROUPS = 2
-W_VECTOR_COLS = 192
+W_VECTOR_COLS = [256, 256, 256, 256]
+LOADS = [(2,), (3,), (4,), (5,)]
+ORDER = [(0, 0), (0, 1), (1, 0), (2, 0), (1, 1), (2, 1)]
 WIDE = [(0, H, t, 1) for t in range(PACK)]
+HALF = [(0, 2, 0, 2), (0, 2, 2, 2), (2, 2, 0, 2), (2, 2, 2, 2)]
 LAST = [(0, 2, 0, 2), (0, 2, 2, 2), (2, 1, 0, PACK), (3, 1, 0, PACK)]
 
 
@@ -46,6 +49,10 @@ def tile_value_cache_projection_g6_kernel(tc, x_words, x_scales, w_v, b_v, out_0
             slot = (group % 2) * PACK + t
             return psum.tile([P, N], F32, name="acc%d_%d" % (group, t), tag="bank%d" % slot)
 
+        def first_token(group):
+            b, half = ORDER[group]
+            return T * b + SPAN * half
+
         def load_scales(raw, first, count):
             for q in range(QUADS):
                 nc.sync.dma_start(
@@ -53,13 +60,13 @@ def tile_value_cache_projection_g6_kernel(tc, x_words, x_scales, w_v, b_v, out_0
                     in_=xs_i32[:, 4 * q : 4 * q + 4, first // 4 : (first + count) // 4],
                 )
 
-        def sort_scales(raw, first, group):
-            out = kept([P, SPAN], U8, "xs%d" % group)
+        def sort_scales(raw, groups, name):
+            out = kept([P, groups, SPAN], U8, name)
             nc.vector.tensor_copy(
-                out=out[:].rearrange("p (t m i) -> p m t i", t=PACK, i=16),
-                in_=raw[:, first : first + SPAN].rearrange("p (m i t) -> p m t i", t=PACK, i=16),
+                out=out[:].rearrange("p n (t m i) -> p n m t i", t=PACK, i=16),
+                in_=raw[:].rearrange("p (n m i t) -> p n m t i", n=groups, t=PACK, i=16),
             )
-            return out
+            return [out[:, n, :] for n in range(groups)]
 
         def sort_words(src, name, passes):
             out = kept([P, passes, SPAN], I32, name)
@@ -76,7 +83,7 @@ def tile_value_cache_projection_g6_kernel(tc, x_words, x_scales, w_v, b_v, out_0
 
         def group_w(raw, g):
             grouped = kept([P, N, PACK], BF16, "w_grouped%d" % g)
-            lo, hi = slice(0, W_VECTOR_COLS), slice(W_VECTOR_COLS, N)
+            lo, hi = slice(0, W_VECTOR_COLS[g]), slice(W_VECTOR_COLS[g], N)
             nc.scalar.copy(
                 out=grouped[:, hi, :].rearrange("p (c i) j -> p c j i", i=4),
                 in_=raw[:, :, hi].rearrange("p j (c i) -> p c j i", i=4),
@@ -117,18 +124,24 @@ def tile_value_cache_projection_g6_kernel(tc, x_words, x_scales, w_v, b_v, out_0
             )
 
         def store_and_round(y, y_bf, group, h0, heads):
-            b, half = divmod(group, HALVES)
+            store_y(y, group, h0, heads)
+            round_y(y, y_bf, h0, heads)
+
+        def store_y(y, group, h0, heads):
+            b, half = ORDER[group]
             nc.sync.dma_start(
                 out=out_0[b, h0 : h0 + heads, SPAN * half : SPAN * (half + 1), :].rearrange("h (p t) c -> p h (t c)", t=PACK),
                 in_=y[:, h0 : h0 + heads, :],
             )
+
+        def round_y(y, y_bf, h0, heads):
             nc.scalar.copy(
                 out=y_bf[:, h0 : h0 + heads, :].rearrange("p h (c i t) -> p h c t i", t=PACK, i=4),
                 in_=y[:, h0 : h0 + heads, :].rearrange("p h (t c i) -> p h c t i", t=PACK, i=4),
             )
 
         def quantize_y(y_bf, codes, group, h0, heads):
-            b, half = divmod(group, HALVES)
+            b, half = ORDER[group]
             nc.vector.quantize_mx(
                 out=codes[:, HD * h0 : HD * (h0 + heads)].bitcast(FP8X4),
                 scales=y_scales[half][:, N * b + HD * h0 : N * b + HD * (h0 + heads)],
@@ -136,7 +149,7 @@ def tile_value_cache_projection_g6_kernel(tc, x_words, x_scales, w_v, b_v, out_0
             )
 
         def store_codes(codes, group, h0, heads):
-            b, half = divmod(group, HALVES)
+            b, half = ORDER[group]
             words = out_1[half].rearrange("p m t -> p (m t)").bitcast(I32)
             nc.sync.dma_start(
                 out=words[:, N * b + HD * h0 : N * b + HD * (h0 + heads)], in_=codes[:, HD * h0 : HD * (h0 + heads)]
@@ -158,97 +171,112 @@ def tile_value_cache_projection_g6_kernel(tc, x_words, x_scales, w_v, b_v, out_0
         make_identity(nc, ident[:])
 
         b_cols = kept([P, PACK], BF16, "b_cols")
-        nc.sync.dma_start(out=b_cols[:], in_=b_v.rearrange("(n j) -> n j", j=PACK))
         w_raw, x_head = [], []
         for g in range(PASSES):
             w_raw.append(load_w(g))
             if g == 0:
+                nc.sync.dma_start(out=b_cols[:], in_=b_v.rearrange("(n j) -> n j", j=PACK))
                 load_scales(xs_head, 0, head_tokens)
             raw = kept([P, head_tokens], I32, "x_head%d" % g)
             nc.sync.dma_start(out=raw[:], in_=x_i32[g][:, 0:head_tokens])
             x_head.append(raw)
         load_scales(xs_rest, head_tokens, B * T - head_tokens)
         x_raw = {}
-        for group in range(HEAD_GROUPS, GROUPS):
-            raw = kept([P, PASSES, SPAN], I32, "x_raw%d" % group)
-            nc.sync.dma_start(out=raw[:], in_=x_all[:, :, SPAN * group : SPAN * (group + 1)])
-            x_raw[group] = raw
+        for groups in LOADS:
+            first = min(first_token(group) for group in groups)
+            raw = kept([P, PASSES, SPAN * len(groups)], I32, "x_raw%d" % groups[0])
+            nc.sync.dma_start(out=raw[:], in_=x_all[:, :, first : first + SPAN * len(groups)])
+            for group in groups:
+                x_raw[group] = raw[:, :, first_token(group) - first : first_token(group) - first + SPAN]
 
         spread = psum.tile([P, PACK, P], BF16, name="spread", tag="bank%d" % (2 * PACK - 1))
         for j in range(PACK):
             nc.tensor.transpose(spread[:, j, :], b_cols[:, j : j + 1].to_broadcast([P, P]), ident[:])
         bias = kept([P, H, HD], F32, "bias")
-        nc.scalar.copy(out=bias[:].rearrange("p h (n j) -> p (h n) j", j=PACK), in_=spread[:].rearrange("p j n -> p n j"))
 
         y_scales = [kept([P, B * N], U8, "y_scales%d" % half) for half in range(HALVES)]
 
-        w_q, x_scale, acc = {}, {}, {}
+        w_q, acc = {}, {}
         for g in range(PASSES):
             grouped = group_w(w_raw[g], g)
             if g == 0:
-                for group in range(HEAD_GROUPS):
-                    x_scale[group] = sort_scales(xs_head, SPAN * group, group)
-            x_pass = [
-                sort_words(x_head[g][:, SPAN * group : SPAN * (group + 1)].unsqueeze(1), "x_sorted%d_%d" % (group, g), 1)
-                for group in range(HEAD_GROUPS)
-            ]
+                nc.scalar.copy(out=bias[:].rearrange("p h (n j) -> p (h n) j", j=PACK), in_=spread[:].rearrange("p j n -> p n j"))
+                x_scale = sort_scales(xs_head, HEAD_GROUPS, "xs_sorted_head")
             w_q[g] = quantize_w(grouped, g)
             for group in range(HEAD_GROUPS):
+                x_pass = sort_words(x_head[g][:, SPAN * group : SPAN * (group + 1)].unsqueeze(1), "x_head_sorted%d_%d" % (g, group), 1)
                 for t in range(PACK):
                     if g == 0:
                         acc[group, t] = bank(group, t)
-                    multiply(acc[group, t], x_pass[group][:, 0, :], x_scale[group], WIDE[t], 0, g)
+                    multiply(acc[group, t], x_pass[:, 0, :], x_scale[group], WIDE[t], 0, g)
 
-        x_sorted = {}
-
-        def prepare(group):
-            x_scale[group] = sort_scales(xs_rest, SPAN * (group - HEAD_GROUPS), group)
-            x_sorted[group] = sort_words(x_raw[group][:], "x_sorted%d" % group, PASSES)
+        def sort_rest():
+            x_scale.extend(sort_scales(xs_rest, GROUPS - HEAD_GROUPS, "xs_sorted_rest"))
 
         def result_tiles(group):
             y = flow.tile([P, H, SPAN], F32, name="y%d" % group, tag="y", bufs=4, align_bytes=64)
             y_bf = flow.tile([P, H, SPAN], BF16, name="y_bf%d" % group, tag="y_bf", bufs=3, align_bytes=64)
             return y, y_bf, kept([P, N], I32, "y_codes%d" % group)
 
-        def finish(group):
-            quantize_y(results[group][1], results[group][2], group, 0, H)
-            store_codes(results[group][2], group, 0, H)
-            if group == GROUPS - 2:
-                store_scales(0)
+        def issue(group, j):
+            acc[group, j] = bank(group, j)
+            for slot in range(pieces[group][j][3]):
+                for g in range(PASSES):
+                    multiply(acc[group, j], x_sorted[group][g], x_scale[first_token(group) // SPAN], pieces[group][j], slot, g)
 
-        prepare(HEAD_GROUPS)
-        results = {}
+        def sort_half(group, u):
+            half_sorted = sort_words(x_raw[group][:, 2 * u : 2 * u + 2, :], "x_sorted%d_%d" % (group, u), 2)
+            x_sorted.setdefault(group, []).extend([half_sorted[:, 0, :], half_sorted[:, 1, :]])
+
+        def finish(group, h0, heads):
+            quantize_y(results[group][1], results[group][2], group, h0, heads)
+            if h0 + heads == H:
+                store_codes(results[group][2], group, 0, H)
+                if ORDER[group] == (B - 1, 0):
+                    store_scales(0)
+
         last = GROUPS - 1
+        pieces = [WIDE] * HEAD_GROUPS + [HALF] * (GROUPS - HEAD_GROUPS - 1) + [LAST]
+        results, x_sorted = {}, {}
+        sort_rest()
         for group in range(last):
             results[group] = result_tiles(group)
             y, y_bf, codes = results[group]
             ahead = group + HEAD_GROUPS
-            for t in range(PACK):
-                add_bias(y, acc[group, t], WIDE[t])
-                if ahead < GROUPS:
-                    acc[ahead, t] = bank(ahead, t)
-                    piece = LAST[t] if ahead == last else WIDE[t]
-                    for slot in range(piece[3]):
-                        for g in range(PASSES):
-                            multiply(acc[ahead, t], x_sorted[ahead][:, g, :], x_scale[ahead], piece, slot, g)
-                if t == 1 and ahead + 1 < GROUPS:
-                    prepare(ahead + 1)
-                if t == 2 and group > 0:
-                    finish(group - 1)
-            store_and_round(y, y_bf, group, 0, H)
+            if group == 0:
+                between = [None, lambda: sort_half(ahead, 0), lambda: sort_half(ahead, 1), None]
+            elif group == 1:
+                between = [lambda: sort_half(ahead, 0), lambda: sort_half(ahead, 1), lambda: finish(0, 0, H), None]
+            elif ahead < GROUPS:
+                between = [lambda: sort_half(ahead, 0), None, lambda: sort_half(ahead, 1), lambda: finish(group - 1, 0, H)]
+            else:
+                between = [lambda: finish(group - 1, 0, 2), None, lambda: finish(group - 1, 2, 2), None]
+            issued = 0
+            for j in range(PACK):
+                add_bias(y, acc[group, j], pieces[group][j])
+                if group >= HEAD_GROUPS and j % 2 == 1:
+                    store_and_round(y, y_bf, group, j - 1, 2)
+                if group < HEAD_GROUPS and j == PACK - 1:
+                    store_and_round(y, y_bf, group, 0, H)
+                if between[j]:
+                    between[j]()
+                if len(x_sorted.get(ahead, [])) == PASSES:
+                    for i in range(issued, j + 1):
+                        issue(ahead, i)
+                    issued = j + 1
 
-        y, y_bf, codes = result_tiles(last)
+        results[last] = result_tiles(last)
+        y, y_bf, codes = results[last]
         add_bias(y, acc[last, 0], LAST[0])
+        finish(last - 1, 0, 2)
         add_bias(y, acc[last, 1], LAST[1])
-        store_and_round(y, y_bf, last, 0, 2)
-        finish(last - 1)
+        round_y(y, y_bf, 0, 2)
+        finish(last - 1, 2, 2)
         add_bias(y, acc[last, 2], LAST[2])
-        store_and_round(y, y_bf, last, 2, 1)
-        quantize_y(y_bf, codes, last, 0, 2)
-        store_codes(codes, last, 0, 2)
+        store_y(y, last, 0, 3)
+        round_y(y, y_bf, 2, 1)
         add_bias(y, acc[last, 3], LAST[3])
         store_and_round(y, y_bf, last, 3, 1)
-        quantize_y(y_bf, codes, last, 2, 1)
-        quantize_y(y_bf, codes, last, 3, 1)
-        store_codes(codes, last, 2, 2)
+        finish(last, 0, 2)
+        finish(last, 2, 2)
         store_scales(1)

from contextlib import ExitStack

import concourse.mybir as mybir
from concourse.masks import make_identity

B, T, D, H, HD = 3, 1024, 2048, 4, 128
N = H * HD
FLOPS = 2 * B * T * D * N

F32 = mybir.dt.float32
BF16 = mybir.dt.bfloat16
I32 = mybir.dt.int32
U8 = mybir.dt.uint8
FP8X4 = mybir.dt.float8_e4m3fn_x4

P = 128
PACK = 4
SPAN = P * PACK
PASSES = D // SPAN
GROUPS = B * T // SPAN
HALVES = T // SPAN
QUADS = 4
HEAD_GROUPS = 2
W_VECTOR_COLS = [256, 256, 256, 256]
LOADS = [(2,), (3,), (4,), (5,)]
ORDER = [(0, 0), (0, 1), (1, 0), (2, 0), (1, 1), (2, 1)]
WIDE = [(0, H, t, 1) for t in range(PACK)]
HALF = [(0, 2, 0, 2), (0, 2, 2, 2), (2, 2, 0, 2), (2, 2, 2, 2)]
LAST = [(0, 2, 0, 2), (0, 2, 2, 2), (2, 1, 0, PACK), (3, 1, 0, PACK)]


def tile_value_cache_projection_g6_kernel(tc, x_words, x_scales, w_v, b_v, out_0, out_1, out_2):
    nc = tc.nc
    x_i32 = [x_words[g].rearrange("p n t -> p (n t)").bitcast(I32) for g in range(PASSES)]
    x_all = x_words.rearrange("g p n t -> p g (n t)").bitcast(I32)
    xs_i32 = x_scales.bitcast(I32)
    head_tokens = HEAD_GROUPS * SPAN

    with ExitStack() as ctx:
        keep = ctx.enter_context(tc.tile_pool(name="keep", bufs=1))
        flow = ctx.enter_context(tc.tile_pool(name="flow", bufs=1))
        psum = ctx.enter_context(tc.psum_pool(name="psum", bufs=1))
        ctx.enter_context(tc.manual_schedule())

        def kept(shape, dtype, name):
            return keep.tile(shape, dtype, name=name, align_bytes=64)

        def bank(group, t):
            slot = (group % 2) * PACK + t
            return psum.tile([P, N], F32, name="acc%d_%d" % (group, t), tag="bank%d" % slot)

        def first_token(group):
            b, half = ORDER[group]
            return T * b + SPAN * half

        def load_scales(raw, first, count):
            for q in range(QUADS):
                nc.sync.dma_start(
                    out=raw[32 * q : 32 * q + 16, :].bitcast(I32),
                    in_=xs_i32[:, 4 * q : 4 * q + 4, first // 4 : (first + count) // 4],
                )

        def sort_scales(raw, groups, name):
            out = kept([P, groups, SPAN], U8, name)
            nc.vector.tensor_copy(
                out=out[:].rearrange("p n (t m i) -> p n m t i", t=PACK, i=16),
                in_=raw[:].rearrange("p (n m i t) -> p n m t i", n=groups, t=PACK, i=16),
            )
            return [out[:, n, :] for n in range(groups)]

        def sort_words(src, name, passes):
            out = kept([P, passes, SPAN], I32, name)
            nc.vector.tensor_copy(
                out=out[:].rearrange("p g (t m i) -> p g m t i", t=PACK, i=2),
                in_=src.rearrange("p g (m i t) -> p g m t i", t=PACK, i=2),
            )
            return out

        def load_w(g):
            raw = kept([P, PACK, N], BF16, "w_raw%d" % g)
            nc.sync.dma_start(out=raw[:], in_=w_v[SPAN * g : SPAN * (g + 1), :].rearrange("(p j) c -> p j c", j=PACK))
            return raw

        def group_w(raw, g):
            grouped = kept([P, N, PACK], BF16, "w_grouped%d" % g)
            lo, hi = slice(0, W_VECTOR_COLS[g]), slice(W_VECTOR_COLS[g], N)
            nc.scalar.copy(
                out=grouped[:, hi, :].rearrange("p (c i) j -> p c j i", i=4),
                in_=raw[:, :, hi].rearrange("p j (c i) -> p c j i", i=4),
            )
            nc.vector.tensor_copy(
                out=grouped[:, lo, :].rearrange("p (c i) j -> p c j i", i=4),
                in_=raw[:, :, lo].rearrange("p j (c i) -> p c j i", i=4),
            )
            return grouped

        def quantize_w(grouped, g):
            codes = kept([P, N], I32, "w_codes%d" % g)
            scales = kept([P, N], U8, "w_scales%d" % g)
            nc.vector.quantize_mx(out=codes[:].bitcast(FP8X4), scales=scales[:], in_=grouped[:].rearrange("p c j -> p (c j)"))
            return codes, scales

        def multiply(acc, x_pass, x_scale, piece, slot, g):
            h0, heads, t0, slots = piece
            tokens = slice(P * (t0 + slot), P * (t0 + slot + 1))
            channels = slice(HD * h0, HD * (h0 + heads))
            nc.tensor.matmul_mx(
                out=acc[:, HD * heads * slot : HD * heads * (slot + 1)],
                lhsT=x_pass[:, tokens].bitcast(FP8X4),
                lhsT_scale=x_scale[4 * g :, tokens],
                rhs=w_q[g][0][:, channels].bitcast(FP8X4),
                rhs_scale=w_q[g][1][:, channels],
                start=(g == 0),
                stop=(g == PASSES - 1),
            )

        def add_bias(y, acc, piece):
            h0, heads, t0, slots = piece
            nc.vector.tensor_tensor(
                out=y[:].rearrange("p h (t c) -> p h t c", t=PACK)[:, h0 : h0 + heads, t0 : t0 + slots, :],
                in0=acc[:].rearrange("p (t h c) -> p h t c", t=slots, h=heads),
                in1=bias[:, h0 : h0 + heads, :].unsqueeze(2).to_broadcast([P, heads, slots, HD]),
                op=mybir.AluOpType.add,
            )

        def store_and_round(y, y_bf, group, h0, heads):
            store_y(y, group, h0, heads)
            round_y(y, y_bf, h0, heads)

        def store_y(y, group, h0, heads):
            b, half = ORDER[group]
            nc.sync.dma_start(
                out=out_0[b, h0 : h0 + heads, SPAN * half : SPAN * (half + 1), :].rearrange("h (p t) c -> p h (t c)", t=PACK),
                in_=y[:, h0 : h0 + heads, :],
            )

        def round_y(y, y_bf, h0, heads):
            nc.scalar.copy(
                out=y_bf[:, h0 : h0 + heads, :].rearrange("p h (c i t) -> p h c t i", t=PACK, i=4),
                in_=y[:, h0 : h0 + heads, :].rearrange("p h (t c i) -> p h c t i", t=PACK, i=4),
            )

        def quantize_y(y_bf, codes, group, h0, heads):
            b, half = ORDER[group]
            nc.vector.quantize_mx(
                out=codes[:, HD * h0 : HD * (h0 + heads)].bitcast(FP8X4),
                scales=y_scales[half][:, N * b + HD * h0 : N * b + HD * (h0 + heads)],
                in_=y_bf[:, h0 : h0 + heads, :].rearrange("p h e -> p (h e)"),
            )

        def store_codes(codes, group, h0, heads):
            b, half = ORDER[group]
            words = out_1[half].rearrange("p m t -> p (m t)").bitcast(I32)
            nc.sync.dma_start(
                out=words[:, N * b + HD * h0 : N * b + HD * (h0 + heads)], in_=codes[:, HD * h0 : HD * (h0 + heads)]
            )

        def store_scales(half):
            for q in range(QUADS):
                queue = nc.scalar if (half == HALVES - 1 and q % 2 == 0) else nc.sync
                queue.dma_start(
                    out=out_2[half, 4 * q : 4 * q + 4, :].bitcast(I32),
                    in_=y_scales[half][32 * q : 32 * q + 4, :].bitcast(I32),
                )

        xs_head = kept([P, head_tokens], U8, "xs_head")
        xs_rest = kept([P, B * T - head_tokens], U8, "xs_rest")
        nc.vector.memset(xs_head[:].bitcast(I32), 0)
        nc.vector.memset(xs_rest[:].bitcast(I32), 0)
        ident = kept([P, P], BF16, "ident")
        make_identity(nc, ident[:])

        b_cols = kept([P, PACK], BF16, "b_cols")
        w_raw, x_head = [], []
        for g in range(PASSES):
            w_raw.append(load_w(g))
            if g == 0:
                nc.sync.dma_start(out=b_cols[:], in_=b_v.rearrange("(n j) -> n j", j=PACK))
                load_scales(xs_head, 0, head_tokens)
            raw = kept([P, head_tokens], I32, "x_head%d" % g)
            nc.sync.dma_start(out=raw[:], in_=x_i32[g][:, 0:head_tokens])
            x_head.append(raw)
        load_scales(xs_rest, head_tokens, B * T - head_tokens)
        x_raw = {}
        for groups in LOADS:
            first = min(first_token(group) for group in groups)
            raw = kept([P, PASSES, SPAN * len(groups)], I32, "x_raw%d" % groups[0])
            nc.sync.dma_start(out=raw[:], in_=x_all[:, :, first : first + SPAN * len(groups)])
            for group in groups:
                x_raw[group] = raw[:, :, first_token(group) - first : first_token(group) - first + SPAN]

        spread = psum.tile([P, PACK, P], BF16, name="spread", tag="bank%d" % (2 * PACK - 1))
        for j in range(PACK):
            nc.tensor.transpose(spread[:, j, :], b_cols[:, j : j + 1].to_broadcast([P, P]), ident[:])
        bias = kept([P, H, HD], F32, "bias")

        y_scales = [kept([P, B * N], U8, "y_scales%d" % half) for half in range(HALVES)]

        w_q, acc = {}, {}
        for g in range(PASSES):
            grouped = group_w(w_raw[g], g)
            if g == 0:
                nc.scalar.copy(out=bias[:].rearrange("p h (n j) -> p (h n) j", j=PACK), in_=spread[:].rearrange("p j n -> p n j"))
                x_scale = sort_scales(xs_head, HEAD_GROUPS, "xs_sorted_head")
            w_q[g] = quantize_w(grouped, g)
            for group in range(HEAD_GROUPS):
                x_pass = sort_words(x_head[g][:, SPAN * group : SPAN * (group + 1)].unsqueeze(1), "x_head_sorted%d_%d" % (g, group), 1)
                for t in range(PACK):
                    if g == 0:
                        acc[group, t] = bank(group, t)
                    multiply(acc[group, t], x_pass[:, 0, :], x_scale[group], WIDE[t], 0, g)

        def sort_rest():
            x_scale.extend(sort_scales(xs_rest, GROUPS - HEAD_GROUPS, "xs_sorted_rest"))

        def result_tiles(group):
            y = flow.tile([P, H, SPAN], F32, name="y%d" % group, tag="y", bufs=4, align_bytes=64)
            y_bf = flow.tile([P, H, SPAN], BF16, name="y_bf%d" % group, tag="y_bf", bufs=3, align_bytes=64)
            return y, y_bf, kept([P, N], I32, "y_codes%d" % group)

        def issue(group, j):
            acc[group, j] = bank(group, j)
            for slot in range(pieces[group][j][3]):
                for g in range(PASSES):
                    multiply(acc[group, j], x_sorted[group][g], x_scale[first_token(group) // SPAN], pieces[group][j], slot, g)

        def sort_half(group, u):
            half_sorted = sort_words(x_raw[group][:, 2 * u : 2 * u + 2, :], "x_sorted%d_%d" % (group, u), 2)
            x_sorted.setdefault(group, []).extend([half_sorted[:, 0, :], half_sorted[:, 1, :]])

        def finish(group, h0, heads):
            quantize_y(results[group][1], results[group][2], group, h0, heads)
            if h0 + heads == H:
                store_codes(results[group][2], group, 0, H)
                if ORDER[group] == (B - 1, 0):
                    store_scales(0)

        last = GROUPS - 1
        pieces = [WIDE] * HEAD_GROUPS + [HALF] * (GROUPS - HEAD_GROUPS - 1) + [LAST]
        results, x_sorted = {}, {}
        sort_rest()
        for group in range(last):
            results[group] = result_tiles(group)
            y, y_bf, codes = results[group]
            ahead = group + HEAD_GROUPS
            if group == 0:
                between = [None, lambda: sort_half(ahead, 0), lambda: sort_half(ahead, 1), None]
            elif group == 1:
                between = [lambda: sort_half(ahead, 0), lambda: sort_half(ahead, 1), lambda: finish(0, 0, H), None]
            elif ahead < GROUPS:
                between = [lambda: sort_half(ahead, 0), None, lambda: sort_half(ahead, 1), lambda: finish(group - 1, 0, H)]
            else:
                between = [lambda: finish(group - 1, 0, 2), None, lambda: finish(group - 1, 2, 2), None]
            issued = 0
            for j in range(PACK):
                add_bias(y, acc[group, j], pieces[group][j])
                if group >= HEAD_GROUPS and j % 2 == 1:
                    store_and_round(y, y_bf, group, j - 1, 2)
                if group < HEAD_GROUPS and j == PACK - 1:
                    store_and_round(y, y_bf, group, 0, H)
                if between[j]:
                    between[j]()
                if len(x_sorted.get(ahead, [])) == PASSES:
                    for i in range(issued, j + 1):
                        issue(ahead, i)
                    issued = j + 1

        results[last] = result_tiles(last)
        y, y_bf, codes = results[last]
        add_bias(y, acc[last, 0], LAST[0])
        finish(last - 1, 0, 2)
        add_bias(y, acc[last, 1], LAST[1])
        round_y(y, y_bf, 0, 2)
        finish(last - 1, 2, 2)
        add_bias(y, acc[last, 2], LAST[2])
        store_y(y, last, 0, 3)
        round_y(y, y_bf, 2, 1)
        add_bias(y, acc[last, 3], LAST[3])
        store_and_round(y, y_bf, last, 3, 1)
        finish(last, 0, 2)
        finish(last, 2, 2)
        store_scales(1)
